import numpy as np
import ml_dtypes


def mxq(x, axis, fmt="e4m3"):
    dtype, down = {"e4m3": (ml_dtypes.float8_e4m3fn, 7), "e5m2": (ml_dtypes.float8_e5m2, 14)}[fmt]
    v = np.moveaxis(np.asarray(x, np.float32).astype(ml_dtypes.bfloat16).astype(np.float64), axis, -1)
    blocks = v.reshape(v.shape[:-1] + (-1, 32))
    amax = np.abs(blocks).max(-1, keepdims=True)
    byte = np.maximum(np.where(amax > 0, np.frexp(amax)[1] - 1 + 127, 0) - down, 1)
    scale = np.exp2(byte - 127.0)
    codes = (blocks / scale).astype(np.float32).astype(dtype).astype(np.float64)
    return np.moveaxis((codes * scale).reshape(v.shape), -1, axis)


WIDE = False


def mx_kscale(k):
    if not WIDE:
        return np.ones(k)
    levels = np.array([10, -10, 5, -5, 0])
    if k % 512:
        return np.exp2(np.random.permutation(np.resize(levels, k // 32))).repeat(32)
    a = np.empty((k // 512, 16))
    for p in range(k // 512):
        a[p, :8] = np.random.permutation(np.resize(levels, 8))
        for g in range(8):
            far = levels[np.abs(levels - a[p, g]) >= 10]
            a[p, g + 8] = far[np.random.randint(len(far))]
    return np.exp2(a.ravel()).repeat(32)


def f64(x):
    return np.asarray(x).astype(np.float64)


def striped(idx):
    return np.tile(idx.reshape(-1, 16).T, (8, 1)).astype(np.uint16)


def unstriped(offs):
    return offs[:16].T.reshape(-1).astype(np.int64)


E2M1 = np.array([0.0, 0.5, 1.0, 1.5, 2.0, 3.0, 4.0, 6.0, -0.0, -0.5, -1.0, -1.5, -2.0, -3.0, -4.0, -6.0])


def pack_weight(w, fmt):
    k, n = w.shape
    w = f64(np.asarray(w, np.float32).astype(ml_dtypes.bfloat16)).reshape(k // 32, 32, n)
    amax = np.abs(w).max(1)
    if fmt == "e4m3":
        byte = np.frexp(amax)[1] - 1 + 127 - 7
    else:
        mant, ex = np.frexp(amax / 6.0)
        byte = np.where(mant > 0.5, ex, ex - 1) + 127
    byte = np.clip(np.where(amax > 0, byte, 1), 1, 254)
    scaled = (w * np.exp2(127.0 - byte)[:, None, :]).reshape(k, n).astype(np.float32)
    by_word = np.ascontiguousarray(scaled.reshape(k // 512, 128, 4, n).transpose(0, 1, 3, 2))
    if fmt == "e4m3":
        words = by_word.astype(ml_dtypes.float8_e4m3fn).view(np.uint8)
    else:
        c = by_word.astype(ml_dtypes.float4_e2m1fn).view(np.uint8) & 0xF
        words = (c[..., 0::2] | (c[..., 1::2] << 4)).reshape(k // 512, 128, 2 * n)
    return np.ascontiguousarray(words), np.ascontiguousarray(byte.astype(np.uint8).reshape(k // 512, 16, n))


def unpack_weight(words, scales, fmt):
    g, _, n = scales.shape
    words = np.ascontiguousarray(words).reshape(g, 128, n, -1)
    if fmt == "e4m3":
        vals = words.view(ml_dtypes.float8_e4m3fn).astype(np.float64)
    else:
        nib = np.empty((g, 128, n, 4), np.uint8)
        nib[..., 0::2] = words & 0xF
        nib[..., 1::2] = words >> 4
        vals = E2M1[nib]
    vals = vals * np.repeat(np.exp2(scales.astype(np.float64) - 127.0), 8, axis=1)[..., None]
    return vals.transpose(0, 1, 3, 2).reshape(g * 512, n)


def gelu(v):
    return 0.5 * v * (1.0 + np.tanh(np.sqrt(2.0 / np.pi) * (v + 0.044715 * v**3)))


def bf(x):
    return np.asarray(x, np.float32).astype(ml_dtypes.bfloat16)

def planes(Y):
    n, m = Y.shape
    b = f64(bf(Y)).reshape(n // 32, 32, m)
    amax = np.abs(b).max(1)
    byte = np.clip(np.where(amax > 0, np.frexp(amax)[1] - 1 + 127 - 7, 1), 1, 254)
    codes = (b * np.exp2(127.0 - byte)[:, None, :]).reshape(n, m).astype(np.float32).astype(ml_dtypes.float8_e4m3fn).view(np.uint8)
    words = codes.reshape(n // 512, 128, 4, m).transpose(0, 1, 3, 2)
    return np.ascontiguousarray(words), np.ascontiguousarray(byte.astype(np.uint8).reshape(n // 512, 16, m))


K, R, H, N, T, S = 1024, 512, 1024, 512, 2048, 512

def setup_inputs():
    n = np.random.standard_normal
    s = mx_kscale(K)[:, None]
    q = mx_kscale(R)[:, None]
    u = mx_kscale(H)[:, None]
    gain = np.exp(0.8 * n(N))
    tab_words, tab_scales = pack_weight(n((K, T)) * s, "e4m3")
    wv_words, wv_scales = pack_weight(n((K, H)) / np.sqrt(K) / s * u.T, "e2m1")
    ws_words, ws_scales = pack_weight(n((K, H)) / np.sqrt(K) / s * u.T, "e4m3")
    return {
        "tab_words": tab_words, "tab_scales": tab_scales,
        "offs": striped(np.random.permutation(T)[:S]),
        "wd": (n((K, R)) / np.sqrt(K) / s * q.T).astype(np.float32),
        "wu": (n((R, H)) * np.sqrt(2.0 / R) / q).astype(np.float32),
        "bu": (0.5 * n(H)).astype(np.float32),
        "wv_words": wv_words, "wv_scales": wv_scales,
        "ws_words": ws_words, "ws_scales": ws_scales,
        "wn": (0.7 * n((H, N)) / np.sqrt(H) / u * gain).astype(np.float32),
        "bn": (0.5 * n(N) * gain).astype(np.float32),
    }

def reference(tab_words, tab_scales, offs, wd, wu, bu, wv_words, wv_scales, ws_words, ws_scales, wn, bn):
    v = unpack_weight(tab_words, tab_scales, "e4m3")[:, unstriped(offs)]
    wv = unpack_weight(wv_words, wv_scales, "e2m1")
    ws = unpack_weight(ws_words, ws_scales, "e4m3")
    d = np.maximum(mxq(f64(wd), 0, "e4m3").T @ v, 0.0)
    up = (mxq(f64(wu), 0, "e4m3").T @ mxq(d, 0, "e4m3")) + f64(bu)[:, None]
    val = wv.T @ v
    skip = ws.T @ v
    h = up * val + skip
    y = (mxq(f64(wn), 0, "e4m3").T @ mxq(h, 0, "e4m3")) + f64(bn)[:, None]
    words, scales = planes(y)
    return y, words, scales

@@ -1,0 +1,354 @@
+import math
+from contextlib import ExitStack
+
+import concourse.mybir as mybir
+from concourse.masks import make_identity
+
+K, R, H, N, T, S = 1024, 512, 1024, 512, 2048, 512
+FLOPS = 2 * S * (K * R + R * H + 2 * K * H + H * N)
+
+F32 = mybir.dt.float32
+BF16 = mybir.dt.bfloat16
+I32 = mybir.dt.int32
+U32 = mybir.dt.uint32
+U16 = mybir.dt.uint16
+U8 = mybir.dt.uint8
+FP8X4 = mybir.dt.float8_e4m3fn_x4
+FP4X4 = mybir.dt.float4_e2m1fn_x4
+ACT = mybir.ActivationFunctionType
+ALU = mybir.AluOpType
+
+P = 128
+KP = 512
+JC = 128
+WU1, WS1, WN = "s", "v", ("s", "s")
+BYTES_OF = {F32: 4, I32: 4, U32: 4, BF16: 2, U8: 1}
+
+
+def tile_list_fraud_lowrank_cross_kernel(
+    tc, tab_words, tab_scales, offs, wd, wu, bu, wv_words, wv_scales, ws_words, ws_scales, wn, bn, out_0, out_1, out_2
+):
+    nc = tc.nc
+    with ExitStack() as ctx:
+        held = ctx.enter_context(tc.tile_pool(name="held", bufs=1))
+        sb = ctx.enter_context(tc.tile_pool(name="sb", bufs=1))
+        ps = ctx.enter_context(tc.psum_pool(name="ps", bufs=1))
+
+        place = {"end": 0}
+
+        def tile(shape, dtype, name, over=None, at=0):
+            if over is None:
+                place[name] = place["end"]
+                place["end"] = place[name] + 64 * math.ceil(math.prod(shape[1:]) * BYTES_OF[dtype] / 64)
+            else:
+                place[name] = place[over] + at
+            return sb.tile(shape, dtype, name=name, align_bytes=64, offset=place[name])
+
+        def copy(eng, out, in_):
+            if eng == "v":
+                nc.vector.tensor_copy(out=out, in_=in_)
+            elif eng == "s":
+                nc.scalar.copy(out=out, in_=in_)
+            else:
+                nc.gpsimd.tensor_scalar(out=out, in0=in_, scalar1=1.0, scalar2=0.0, op0=ALU.mult, op1=ALU.add)
+
+        def move(eng, out, in_):
+            if eng == "v":
+                nc.vector.tensor_copy(out=out.bitcast(I32), in_=in_.bitcast(I32))
+            else:
+                nc.scalar.copy(out=out.bitcast(U32), in_=in_.bitcast(U32))
+
+        def quantize(codes, scales, in_):
+            nc.vector.quantize_mx(out=codes.bitcast(FP8X4), scales=scales, in_=in_)
+
+        offsets = held.tile([P, S // 16], U16, name="offsets")
+        nc.sync.dma_start(offsets[:], offs)
+
+        tab_sc = tile([P, 2 * T], U8, "tab_sc")
+        w_sc_raw = tile([P, 2 * H], U8, "w_sc_raw")
+        w_sc = tile([P, 2 * H], U8, "w_sc")
+        nc.vector.memset(tab_sc[:].bitcast(I32), 0)
+        nc.vector.memset(w_sc[:].bitcast(I32), 0)
+
+        def load_scales(queue, dst, row0, src):
+            for q in range(4):
+                queue.dma_start(
+                    out=dst[32 * q + row0 : 32 * q + row0 + 4, :].bitcast(I32).rearrange("r (a n) -> r a n", a=2),
+                    in_=src[:, 4 * q : 4 * q + 4, :].bitcast(I32).rearrange("a r n -> r a n"),
+                )
+
+        tab_sc_raw = tile([P, 2 * T], U8, "tab_sc_raw")
+        load_scales(nc.sync, tab_sc_raw, 0, tab_scales)
+        wd_raw = [tile([P, 4, R], F32, f"wd_raw{a}") for a in range(2)]
+        for a in range(2):
+            nc.sync.dma_start(out=wd_raw[a][:], in_=wd[KP * a : KP * (a + 1), :].rearrange("(p j) c -> p j c", j=4))
+            if a == 0:
+                load_scales(nc.sync, w_sc_raw, 0, wv_scales)
+        load_scales(nc.sync, w_sc_raw, 4, ws_scales)
+        tab_w = [tile([P, T], U32, f"tab_w{a}") for a in range(2)]
+        for a in range(2):
+            nc.sync.dma_start(out=tab_w[a][:].bitcast(I32), in_=tab_words[a].rearrange("p n t -> p (n t)").bitcast(I32))
+
+        bu_rows = tile([P, 2 * P], F32, "bu_rows")
+        nc.gpsimd.memset(bu_rows[:], 0.0)
+        nc.scalar.dma_start(
+            out=bu_rows[0:4, :].rearrange("t (g i) -> t g i", i=8), in_=bu.rearrange("(g t i) -> t g i", t=4, i=8)
+        )
+        ident = tile([P, P], F32, "ident")
+        make_identity(nc, ident[:])
+        bn_sb = tile([P, 4], F32, "bn_sb")
+        nc.gpsimd.dma_start(out=bn_sb[:], in_=bn.rearrange("(p t) -> p t", t=4))
+
+        wu_raw = [tile([P, 4, KP], F32, f"wu_raw{b}") for b in range(2)]
+        wv_raw = [tile([P, 2, KP // 2], U32, f"wv_raw{b}") for b in range(2)]
+        ws_raw = [tile([P, 2, KP], U32, f"ws_raw{b}") for b in range(2)]
+        for b in range(2):
+            nc.sync.dma_start(out=wu_raw[b][:], in_=wu.rearrange("(p j) c -> p j c", j=4)[:, :, KP * b : KP * (b + 1)])
+            nc.sync.dma_start(
+                out=wv_raw[b][:].bitcast(I32),
+                in_=wv_words[:, :, 2 * KP * b : 2 * KP * (b + 1)].bitcast(I32).rearrange("a p n -> p a n"),
+            )
+            nc.sync.dma_start(
+                out=ws_raw[b][:].bitcast(I32),
+                in_=ws_words[:, :, KP * b : KP * (b + 1), :].rearrange("a p n t -> p a (n t)").bitcast(I32),
+            )
+        wn_raw = [tile([P, 4, N], F32, f"wn_raw{b}") for b in range(2)]
+        for b in range(2):
+            rows = wn[KP * b : KP * (b + 1), :].rearrange("(g t i) n -> t g i n", t=4, i=8)
+            for t in range(4):
+                nc.sync.dma_start(out=wn_raw[b][:, t, :], in_=rows[t])
+
+        bu_ps = ps.tile([P, 2, P], F32, name="bu_ps", tag="skip", bufs=2)
+        for b in range(2):
+            nc.tensor.transpose(bu_ps[:, b, :], bu_rows[:, P * b : P * (b + 1)], ident[:])
+        bu_sb = tile([P, 2, 4], F32, "bu_sb")
+        nc.scalar.activation(out=bu_sb[:], in_=bu_ps[:, :, 0:4], func=ACT.Copy)
+
+        def dealt_weight(engs, raw, name, over=None, at=0):
+            grouped = tile([P, 4 * KP], BF16, name + "_bf", over, at)
+            dst = grouped[:].rearrange("p (u v m j) -> p u m j v", u=2, v=2, j=4)
+            src = raw[:].rearrange("p j (m u v) -> p u m j v", u=2, v=2)
+            if len(engs) == 1:
+                copy(engs, dst, src)
+            else:
+                for u in range(2):
+                    copy(engs[u], dst[:, u], src[:, u])
+            return grouped
+
+        def quantize_whole(grouped, name):
+            codes = tile([P, KP], U32, name + "_q")
+            scales = tile([P, KP], U8, name + "_s")
+            quantize(codes[:], scales[:], grouped[:])
+            return codes, scales
+
+        for q in range(4):
+            live = slice(32 * q, 32 * q + 4)
+            nc.vector.tensor_copy(out=tab_sc[live, :].bitcast(I32), in_=tab_sc_raw[live, :].bitcast(I32))
+        g_sc = [tile([P, S], U8, f"g_sc{a}") for a in range(2)]
+        for a in range(2):
+            nc.vector.tensor_copy(g_sc[a][:], tab_sc[:, T * a : T * (a + 1)].indirect(offsets[:]))
+        for q in range(4):
+            live = slice(32 * q, 32 * q + 8)
+            nc.vector.tensor_copy(
+                out=w_sc[live, :].bitcast(I32).rearrange("p (e t g i) -> p e t g i", t=4, g=16, i=2),
+                in_=w_sc_raw[live, :].bitcast(I32).rearrange("p (e g t i) -> p e t g i", t=4, g=16, i=2),
+            )
+        wd_bf = [dealt_weight("s", wd_raw[0], "wd0"), dealt_weight("sv", wd_raw[1], "wd1")]
+        wd_q = [quantize_whole(wd_bf[a], f"wd{a}") for a in range(2)]
+
+        g_w = [tile([P, S], U32, f"g_w{a}") for a in range(2)]
+        for a in range(2):
+            for half in range(2):
+                nc.vector.tensor_copy(
+                    g_w[a][:, 256 * half : 256 * (half + 1)],
+                    tab_w[a][:].indirect(offsets[:, 16 * half : 16 * (half + 1)]),
+                )
+
+        def mm(out, lhs, lhs_s, rhs, rhs_s, start, stop, lhs_dt=FP8X4):
+            nc.tensor.matmul_mx(
+                out=out, lhsT=lhs.bitcast(lhs_dt), lhsT_scale=lhs_s, rhs=rhs.bitcast(FP8X4), rhs_scale=rhs_s,
+                start=start, stop=stop,
+            )
+
+        def jcols(jc, width=JC):
+            return slice(width * jc, width * (jc + 1))
+
+        d_ps = [ps.tile([P, 4, JC], F32, name=f"d_ps{jc}", tag="dy", bufs=4) for jc in range(4)]
+        for a in range(2):
+            for jc in range(4):
+                for t in range(4):
+                    mm(d_ps[jc][:, t, :], wd_q[a][0][:, jcols(t)], wd_q[a][1][:, jcols(t)],
+                       g_w[a][:, jcols(jc)], g_sc[a][:, jcols(jc)], a == 0 and t == 0, a == 1 and t == 3)
+        d_bf = [tile([P, 8 * JC], BF16, f"d_bf{half}") for half in range(2)]
+        for jc in range(4):
+            nc.scalar.activation(
+                out=d_bf[jc // 2][:, jcols(jc % 2, 4 * JC)].rearrange("p (j t) -> p j t", t=4), in_=d_ps[jc][:].rearrange("p t j -> p j t"),
+                func=ACT.Relu,
+            )
+        d_q = tile([P, S], U32, "d_q")
+        d_s = tile([P, S], U8, "d_s")
+
+        def quantize_d(half):
+            quantize(d_q[:, jcols(half, 256)], d_s[:, jcols(half, 256)], d_bf[half][:])
+
+        wu_q = [tile([P, KP], U32, f"wu_q{b}") for b in range(2)]
+        wu_s = [tile([P, KP], U8, f"wu_s{b}") for b in range(2)]
+        val = [[tile([P, S], F32, f"val{b}{t}") for t in range(4)] for b in range(2)]
+        wu_bf = [
+            [tile([P, 2 * KP], BF16, f"wu_bf0{u}", "tab_w1", 2048 * u) for u in range(2)],
+            [tile([P, 2 * KP], BF16, f"wu_bf1{u}", f"val0{u}") for u in range(2)],
+        ]
+
+        def cast_wu(eng, b, t):
+            copy(
+                eng,
+                wu_bf[b][t // 2][:, jcols(t % 2, KP)].rearrange("p (g u v j) -> p g u j v", u=4, v=2, j=4),
+                wu_raw[b][:].rearrange("p j (g t i) -> p t g j i", t=4, i=8)[:, t].rearrange("p g j (u v) -> p g u j v", v=2),
+            )
+
+        def quantize_wu(b, u):
+            quantize(wu_q[b][:, jcols(u, 256)], wu_s[b][:, jcols(u, 256)], wu_bf[b][u][:])
+
+        wv_p = [tile([P, 4 * KP], U8, "wv_p0", "tab_w1", 4096), tile([P, 4 * KP], U8, "wv_p1", "val02")]
+        ws_p = [tile([P, 2 * KP], U32, f"ws_p{b}", "wu_bf00") for b in range(2)]
+
+        def deal_wv(eng, b):
+            move(eng, wv_p[b][:].bitcast(U32).rearrange("p (a t g i) -> p a t g i", a=2, t=4, i=4),
+                 wv_raw[b][:].rearrange("p a (g t i) -> p a t g i", t=4, i=4))
+
+        def deal_ws(eng, b):
+            move(eng, ws_p[b][:].rearrange("p (a t g i) -> p a t g i", a=2, t=4, i=8),
+                 ws_raw[b][:].rearrange("p a (g t i) -> p a t g i", t=4, i=8))
+
+        def value(b, t):
+            acc = ps.tile([P, S], F32, name=f"val_ps{b}{t}", tag="dy", bufs=4)
+            for a in range(2):
+                c0 = KP * a + JC * t
+                s0 = H * a + KP * b + JC * t
+                mm(acc[:], wv_p[b][:, 2 * c0 : 2 * (c0 + JC)], w_sc[:, s0 : s0 + JC], g_w[a][:], g_sc[a][:],
+                   a == 0, a == 1, lhs_dt=FP4X4)
+            nc.scalar.copy(out=val[b][t][:], in_=acc[:])
+
+        def cross(b, t, j0, width, dst):
+            cols = slice(j0, j0 + width)
+            acc = ps.tile([P, width], F32, name=f"up_ps{b}{t}{j0}", tag="uv", bufs=2)
+            mm(acc[:], wu_q[b][:, jcols(t)], wu_s[b][:, jcols(t)], d_q[:, cols], d_s[:, cols], True, True)
+            nc.vector.scalar_tensor_tensor(
+                out=dst[:, t, :], in0=acc[:], scalar=bu_sb[:, b, t : t + 1], in1=val[b][t][:, cols],
+                op0=ALU.add, op1=ALU.mult,
+            )
+
+        h_bf = [[tile([P, 8 * JC], BF16, f"h_bf{b}{half}") for half in range(2)] for b in range(2)]
+        h_q = [tile([P, S], U32, f"h_q{b}") for b in range(2)]
+        h_s = [tile([P, S], U8, f"h_s{b}") for b in range(2)]
+
+        def add_skip(b, jc, src):
+            acc = ps.tile([P, 4, JC], F32, name=f"skip_ps{b}{jc}", tag="skip", bufs=2)
+            for t in range(4):
+                for a in range(2):
+                    c0 = KP * a + JC * t
+                    s0 = H * a + KP * b + JC * t
+                    mm(acc[:, t, :], ws_p[b][:, c0 : c0 + JC], w_sc[4:P, s0 : s0 + JC], g_w[a][:, jcols(jc)],
+                       g_sc[a][:, jcols(jc)], a == 0, a == 1)
+            nc.vector.tensor_tensor(
+                out=h_bf[b][jc // 2][:, jcols(jc % 2, 4 * JC)].rearrange("p (c i t) -> p c t i", i=2, t=4),
+                in0=acc[:].rearrange("p t (c i) -> p c t i", i=2),
+                in1=src.rearrange("p t (c i) -> p c t i", i=2),
+                op=ALU.add,
+            )
+
+        def quantize_h(b, jc, n):
+            cols = slice(JC * jc, JC * (jc + n))
+            first = 4 * JC * (jc % 2)
+            quantize(h_q[b][:, cols], h_s[b][:, cols], h_bf[b][jc // 2][:, first : first + 4 * JC * n])
+
+        cast_wu("v", 0, 0)
+        cast_wu("v", 0, 1)
+        quantize_d(0)
+        quantize_wu(0, 0)
+        deal_wv("v", 0)
+        cast_wu("v", 0, 2)
+        cast_wu("v", 0, 3)
+        quantize_d(1)
+        quantize_wu(0, 1)
+        deal_ws("v", 0)
+
+        prod = [tile([P, 4, S], F32, f"prod{b}") for b in range(2)]
+        for t in range(4):
+            value(0, t)
+            cross(0, t, 0, S, prod[0])
+        for t in range(4):
+            cast_wu(WU1, 1, t)
+        deal_wv("s", 1)
+        for jc in range(4):
+            add_skip(0, jc, prod[0][:, :, jcols(jc)])
+            if jc == 2:
+                quantize_h(0, 0, 2)
+            if jc % 2 == 1:
+                quantize_wu(1, jc // 2)
+            value(1, jc)
+        deal_ws(WS1, 1)
+        quantize_h(0, 2, 2)
+
+        wn_bf = [dealt_weight(WN[b], wn_raw[b], f"wn{b}", "prod0", 4096 * b) for b in range(2)]
+        for t in range(4):
+            cross(1, t, 0, S, prod[1])
+        wn_q = [quantize_whole(wn_bf[0], "wn0")]
+        add_skip(1, 0, prod[1][:, :, jcols(0)])
+        add_skip(1, 1, prod[1][:, :, jcols(1)])
+        wn_q.append(quantize_whole(wn_bf[1], "wn1"))
+        quantize_h(1, 0, 2)
+
+        y_sb = [tile([P, 4, S // 2], F32, f"y_sb{half}") for half in range(2)]
+        y_bf = [tile([P, 8 * JC], BF16, f"y_bf{half}") for half in range(2)]
+        y_q = tile([P, S], U32, "y_q")
+        y_s = tile([P, S], U8, "y_s")
+        out_rows = out_0.rearrange("(p t) j -> p t j", t=4)
+        out_words = out_1[0].rearrange("p m t -> p (m t)").bitcast(I32)
+
+        def project(jc, n):
+            cols = slice(JC * jc, JC * (jc + n))
+            first = JC * (jc % 2)
+            per_bank = 4 // n
+            for t0 in range(0, 4, per_bank):
+                acc = ps.tile([P, per_bank, JC * n], F32, name=f"y_ps{jc}{t0}", tag="dy", bufs=4)
+                for b in range(2):
+                    for k in range(per_bank):
+                        mm(acc[:, k, :], wn_q[b][0][:, jcols(t0 + k)], wn_q[b][1][:, jcols(t0 + k)], h_q[b][:, cols],
+                           h_s[b][:, cols], b == 0 and k == 0, b == 1 and k == per_bank - 1)
+                for k in range(per_bank):
+                    nc.scalar.activation(
+                        out=y_sb[jc // 2][:, t0 + k, first : first + JC * n], in_=acc[:, k, :], func=ACT.Identity,
+                        bias=bn_sb[:, t0 + k : t0 + k + 1],
+                    )
+            nc.sync.dma_start(out=out_rows[:, :, cols], in_=y_sb[jc // 2][:, :, first : first + JC * n])
+
+        def round_y(jc, n):
+            first = JC * (jc % 2)
+            nc.vector.tensor_copy(
+                out=y_bf[jc // 2][:, 4 * first : 4 * (first + JC * n)].rearrange("p (c i t) -> p c t i", i=2, t=4),
+                in_=y_sb[jc // 2][:, :, first : first + JC * n].rearrange("p t (c i) -> p c t i", i=2),
+            )
+
+        def quantize_y(jc, n):
+            cols = slice(JC * jc, JC * (jc + n))
+            first = 4 * JC * (jc % 2)
+            quantize(y_q[:, cols], y_s[:, cols], y_bf[jc // 2][:, first : first + 4 * JC * n])
+
+        project(0, 2)
+        add_skip(1, 2, prod[1][:, :, jcols(2)])
+        add_skip(1, 3, prod[1][:, :, jcols(3)])
+        quantize_h(1, 2, 1)
+        quantize_h(1, 3, 1)
+        project(2, 1)
+        project(3, 1)
+        round_y(0, 2)
+        quantize_y(0, 2)
+        nc.sync.dma_start(out=out_words[:, jcols(0, 256)], in_=y_q[:, jcols(0, 256)].bitcast(I32))
+        round_y(2, 1)
+        round_y(3, 1)
+        quantize_y(2, 2)
+        nc.scalar.dma_start(out=out_words[:, jcols(1, 256)], in_=y_q[:, jcols(1, 256)].bitcast(I32))
+        for q in range(4):
+            queue = nc.scalar if q % 2 == 0 else nc.sync
+            queue.dma_start(out=out_2[0, 4 * q : 4 * q + 4, :].bitcast(I32), in_=y_s[32 * q : 32 * q + 4, :].bitcast(I32))

@@ -71,20 +71,19 @@ def tile_list_fraud_lowrank_cross_kernel(
         nc.vector.memset(w_sc[:].bitcast(I32), 0)
 
         def load_scales(queue, dst, row0, src):
-            for q in range(4):
+            for r in range(4):
                 queue.dma_start(
-                    out=dst[32 * q + row0 : 32 * q + row0 + 4, :].bitcast(I32).rearrange("r (a n) -> r a n", a=2),
-                    in_=src[:, 4 * q : 4 * q + 4, :].bitcast(I32).rearrange("a r n -> r a n"),
+                    out=dst[row0 + r : P : 32, :].bitcast(I32).rearrange("q (a n) -> q a n", a=2),
+                    in_=src.bitcast(I32).rearrange("a (q r) n -> r q a n", r=4)[r],
                 )
 
         tab_sc_raw = tile([P, 2 * T], U8, "tab_sc_raw")
         load_scales(nc.sync, tab_sc_raw, 0, tab_scales)
+        load_scales(nc.scalar, w_sc_raw, 4, ws_scales)
+        load_scales(nc.sync, w_sc_raw, 0, wv_scales)
         wd_raw = [tile([P, 4, R], F32, f"wd_raw{a}") for a in range(2)]
         for a in range(2):
             nc.sync.dma_start(out=wd_raw[a][:], in_=wd[KP * a : KP * (a + 1), :].rearrange("(p j) c -> p j c", j=4))
-            if a == 0:
-                load_scales(nc.sync, w_sc_raw, 0, wv_scales)
-        load_scales(nc.sync, w_sc_raw, 4, ws_scales)
         tab_w = [tile([P, T], U32, f"tab_w{a}") for a in range(2)]
         for a in range(2):
             nc.sync.dma_start(out=tab_w[a][:].bitcast(I32), in_=tab_words[a].rearrange("p n t -> p (n t)").bitcast(I32))
@@ -99,15 +98,21 @@ def tile_list_fraud_lowrank_cross_kernel(
         bn_sb = tile([P, 4], F32, "bn_sb")
         nc.gpsimd.dma_start(out=bn_sb[:], in_=bn.rearrange("(p t) -> p t", t=4))
 
-        wu_raw = [tile([P, 4, KP], F32, f"wu_raw{b}") for b in range(2)]
+        wu_raw0 = [tile([P, 4, KP // 2], F32, f"wu_raw0{half}") for half in range(2)]
+        wu_raw1 = tile([P, 4, KP], F32, "wu_raw1")
+        wu_rows = wu.rearrange("(p j) c -> p j c", j=4)
         wv_raw = [tile([P, 2, KP // 2], U32, f"wv_raw{b}") for b in range(2)]
         ws_raw = [tile([P, 2, KP], U32, f"ws_raw{b}") for b in range(2)]
         for b in range(2):
-            nc.sync.dma_start(out=wu_raw[b][:], in_=wu.rearrange("(p j) c -> p j c", j=4)[:, :, KP * b : KP * (b + 1)])
             nc.sync.dma_start(
                 out=wv_raw[b][:].bitcast(I32),
                 in_=wv_words[:, :, 2 * KP * b : 2 * KP * (b + 1)].bitcast(I32).rearrange("a p n -> p a n"),
             )
+            if b == 0:
+                for half in range(2):
+                    nc.sync.dma_start(out=wu_raw0[half][:], in_=wu_rows[:, :, 256 * half : 256 * (half + 1)])
+            else:
+                nc.sync.dma_start(out=wu_raw1[:], in_=wu_rows[:, :, KP:])
             nc.sync.dma_start(
                 out=ws_raw[b][:].bitcast(I32),
                 in_=ws_words[:, :, KP * b : KP * (b + 1), :].rearrange("a p n t -> p a (n t)").bitcast(I32),
@@ -118,7 +123,7 @@ def tile_list_fraud_lowrank_cross_kernel(
             for t in range(4):
                 nc.sync.dma_start(out=wn_raw[b][:, t, :], in_=rows[t])
 
-        bu_ps = ps.tile([P, 2, P], F32, name="bu_ps", tag="skip", bufs=2)
+        bu_ps = ps.tile([P, 2, P], F32, name="bu_ps", tag="ring", bufs=4)
         for b in range(2):
             nc.tensor.transpose(bu_ps[:, b, :], bu_rows[:, P * b : P * (b + 1)], ident[:])
         bu_sb = tile([P, 2, 4], F32, "bu_sb")
@@ -196,21 +201,27 @@ def tile_list_fraud_lowrank_cross_kernel(
         val = [[tile([P, S], F32, f"val{b}{t}") for t in range(4)] for b in range(2)]
         wu_bf = [
             [tile([P, 2 * KP], BF16, f"wu_bf0{u}", "tab_w1", 2048 * u) for u in range(2)],
-            [tile([P, 2 * KP], BF16, f"wu_bf1{u}", f"val0{u}") for u in range(2)],
+            [tile([P, 2 * KP], BF16, f"wu_bf1{u}", f"val0{u + 1}") for u in range(2)],
         ]
 
         def cast_wu(eng, b, t):
             copy(
                 eng,
                 wu_bf[b][t // 2][:, jcols(t % 2, KP)].rearrange("p (g u v j) -> p g u j v", u=4, v=2, j=4),
-                wu_raw[b][:].rearrange("p j (g t i) -> p t g j i", t=4, i=8)[:, t].rearrange("p g j (u v) -> p g u j v", v=2),
+                wu_raw1[:].rearrange("p j (g t i) -> p t g j i", t=4, i=8)[:, t].rearrange("p g j (u v) -> p g u j v", v=2),
+            )
+
+        def cast_wu0(half, u):
+            nc.vector.tensor_copy(
+                out=wu_bf[0][u][:].rearrange("p (v h g i j) -> p h v g i j", v=2, h=2, i=8, j=4)[:, half],
+                in_=wu_raw0[half][:].rearrange("p j (g u v i) -> p u v g i j", u=2, v=2, i=8)[:, u],
             )
 
         def quantize_wu(b, u):
             quantize(wu_q[b][:, jcols(u, 256)], wu_s[b][:, jcols(u, 256)], wu_bf[b][u][:])
 
-        wv_p = [tile([P, 4 * KP], U8, "wv_p0", "tab_w1", 4096), tile([P, 4 * KP], U8, "wv_p1", "val02")]
-        ws_p = [tile([P, 2 * KP], U32, f"ws_p{b}", "wu_bf00") for b in range(2)]
+        wv_p = [tile([P, 4 * KP], U8, "wv_p0", "tab_w1", 4096), tile([P, 4 * KP], U8, "wv_p1", "val00")]
+        ws_p = [tile([P, 2 * KP], U32, f"ws_p{b}", "d_bf0") for b in range(2)]
 
         def deal_wv(eng, b):
             move(eng, wv_p[b][:].bitcast(U32).rearrange("p (a t g i) -> p a t g i", a=2, t=4, i=4),
@@ -231,7 +242,7 @@ def tile_list_fraud_lowrank_cross_kernel(
 
         def cross(b, t, j0, width, dst):
             cols = slice(j0, j0 + width)
-            acc = ps.tile([P, width], F32, name=f"up_ps{b}{t}{j0}", tag="uv", bufs=2)
+            acc = ps.tile([P, width], F32, name=f"up_ps{b}{t}{j0}", tag="ring", bufs=4)
             mm(acc[:], wu_q[b][:, jcols(t)], wu_s[b][:, jcols(t)], d_q[:, cols], d_s[:, cols], True, True)
             nc.vector.scalar_tensor_tensor(
                 out=dst[:, t, :], in0=acc[:], scalar=bu_sb[:, b, t : t + 1], in1=val[b][t][:, cols],
@@ -243,7 +254,7 @@ def tile_list_fraud_lowrank_cross_kernel(
         h_s = [tile([P, S], U8, f"h_s{b}") for b in range(2)]
 
         def add_skip(b, jc, src):
-            acc = ps.tile([P, 4, JC], F32, name=f"skip_ps{b}{jc}", tag="skip", bufs=2)
+            acc = ps.tile([P, 4, JC], F32, name=f"skip_ps{b}{jc}", tag="ring", bufs=4)
             for t in range(4):
                 for a in range(2):
                     c0 = KP * a + JC * t
@@ -262,13 +273,13 @@ def tile_list_fraud_lowrank_cross_kernel(
             first = 4 * JC * (jc % 2)
             quantize(h_q[b][:, cols], h_s[b][:, cols], h_bf[b][jc // 2][:, first : first + 4 * JC * n])
 
-        cast_wu("v", 0, 0)
-        cast_wu("v", 0, 1)
-        quantize_d(0)
-        quantize_wu(0, 0)
         deal_wv("v", 0)
-        cast_wu("v", 0, 2)
-        cast_wu("v", 0, 3)
+        cast_wu0(0, 0)
+        cast_wu0(0, 1)
+        quantize_d(0)
+        cast_wu0(1, 0)
+        cast_wu0(1, 1)
+        quantize_wu(0, 0)
         quantize_d(1)
         quantize_wu(0, 1)
         deal_ws("v", 0)
@@ -277,9 +288,9 @@ def tile_list_fraud_lowrank_cross_kernel(
         for t in range(4):
             value(0, t)
             cross(0, t, 0, S, prod[0])
+        deal_wv("s", 1)
         for t in range(4):
             cast_wu(WU1, 1, t)
-        deal_wv("s", 1)
         for jc in range(4):
             add_skip(0, jc, prod[0][:, :, jcols(jc)])
             if jc == 2:
@@ -298,6 +309,7 @@ def tile_list_fraud_lowrank_cross_kernel(
         add_skip(1, 1, prod[1][:, :, jcols(1)])
         wn_q.append(quantize_whole(wn_bf[1], "wn1"))
         quantize_h(1, 0, 2)
+        add_skip(1, 2, prod[1][:, :, jcols(2)])
 
         y_sb = [tile([P, 4, S // 2], F32, f"y_sb{half}") for half in range(2)]
         y_bf = [tile([P, 8 * JC], BF16, f"y_bf{half}") for half in range(2)]
@@ -336,19 +348,21 @@ def tile_list_fraud_lowrank_cross_kernel(
             quantize(y_q[:, cols], y_s[:, cols], y_bf[jc // 2][:, first : first + 4 * JC * n])
 
         project(0, 2)
-        add_skip(1, 2, prod[1][:, :, jcols(2)])
-        add_skip(1, 3, prod[1][:, :, jcols(3)])
         quantize_h(1, 2, 1)
-        quantize_h(1, 3, 1)
         project(2, 1)
+        add_skip(1, 3, prod[1][:, :, jcols(3)])
+        quantize_h(1, 3, 1)
         project(3, 1)
         round_y(0, 2)
         quantize_y(0, 2)
         nc.sync.dma_start(out=out_words[:, jcols(0, 256)], in_=y_q[:, jcols(0, 256)].bitcast(I32))
         round_y(2, 1)
+        quantize_y(2, 1)
         round_y(3, 1)
-        quantize_y(2, 2)
+        quantize_y(3, 1)
         nc.scalar.dma_start(out=out_words[:, jcols(1, 256)], in_=y_q[:, jcols(1, 256)].bitcast(I32))
         for q in range(4):
             queue = nc.scalar if q % 2 == 0 else nc.sync
-            queue.dma_start(out=out_2[0, 4 * q : 4 * q + 4, :].bitcast(I32), in_=y_s[32 * q : 32 * q + 4, :].bitcast(I32))
+            queue.dma_start(
+                out=out_2[0].bitcast(I32).rearrange("(q r) n -> r q n", r=4)[q], in_=y_s[q:P:32, :].bitcast(I32)
+            )

@@ -68,7 +68,7 @@ def tile_list_fraud_lowrank_cross_kernel(
         w_sc_raw = tile([P, 2 * H], U8, "w_sc_raw")
         w_sc = tile([P, 2 * H], U8, "w_sc")
         nc.vector.memset(tab_sc[:].bitcast(I32), 0)
-        nc.vector.memset(w_sc[:].bitcast(I32), 0)
+        nc.vector.memset(w_sc_raw[:].bitcast(I32), 0)
 
         def load_scales(queue, dst, row0, src):
             for r in range(4):
@@ -79,8 +79,6 @@ def tile_list_fraud_lowrank_cross_kernel(
 
         tab_sc_raw = tile([P, 2 * T], U8, "tab_sc_raw")
         load_scales(nc.sync, tab_sc_raw, 0, tab_scales)
-        load_scales(nc.scalar, w_sc_raw, 4, ws_scales)
-        load_scales(nc.sync, w_sc_raw, 0, wv_scales)
         wd_raw = [tile([P, 4, R], F32, f"wd_raw{a}") for a in range(2)]
         for a in range(2):
             nc.sync.dma_start(out=wd_raw[a][:], in_=wd[KP * a : KP * (a + 1), :].rearrange("(p j) c -> p j c", j=4))
@@ -95,6 +93,8 @@ def tile_list_fraud_lowrank_cross_kernel(
         )
         ident = tile([P, P], F32, "ident")
         make_identity(nc, ident[:])
+        load_scales(nc.gpsimd, w_sc_raw, 0, wv_scales)
+        load_scales(nc.gpsimd, w_sc_raw, 4, ws_scales)
         bn_sb = tile([P, 4], F32, "bn_sb")
         nc.gpsimd.dma_start(out=bn_sb[:], in_=bn.rearrange("(p t) -> p t", t=4))
 
@@ -152,12 +152,6 @@ def tile_list_fraud_lowrank_cross_kernel(
         g_sc = [tile([P, S], U8, f"g_sc{a}") for a in range(2)]
         for a in range(2):
             nc.vector.tensor_copy(g_sc[a][:], tab_sc[:, T * a : T * (a + 1)].indirect(offsets[:]))
-        for q in range(4):
-            live = slice(32 * q, 32 * q + 8)
-            nc.vector.tensor_copy(
-                out=w_sc[live, :].bitcast(I32).rearrange("p (e t g i) -> p e t g i", t=4, g=16, i=2),
-                in_=w_sc_raw[live, :].bitcast(I32).rearrange("p (e g t i) -> p e t g i", t=4, g=16, i=2),
-            )
         wd_bf = [dealt_weight("s", wd_raw[0], "wd0"), dealt_weight("sv", wd_raw[1], "wd1")]
         wd_q = [quantize_whole(wd_bf[a], f"wd{a}") for a in range(2)]
 
@@ -168,6 +162,11 @@ def tile_list_fraud_lowrank_cross_kernel(
                     g_w[a][:, 256 * half : 256 * (half + 1)],
                     tab_w[a][:].indirect(offsets[:, 16 * half : 16 * (half + 1)]),
                 )
+
+        nc.vector.tensor_copy(
+            out=w_sc[:].bitcast(I32).rearrange("p (e t g i) -> p e t g i", t=4, g=16, i=2),
+            in_=w_sc_raw[:].bitcast(I32).rearrange("p (e g t i) -> p e t g i", t=4, g=16, i=2),
+        )
 
         def mm(out, lhs, lhs_s, rhs, rhs_s, start, stop, lhs_dt=FP8X4):
             nc.tensor.matmul_mx(
@@ -318,10 +317,9 @@ def tile_list_fraud_lowrank_cross_kernel(
         out_rows = out_0.rearrange("(p t) j -> p t j", t=4)
         out_words = out_1[0].rearrange("p m t -> p (m t)").bitcast(I32)
 
-        def project(jc, n):
+        def project(jc, n, per_bank):
             cols = slice(JC * jc, JC * (jc + n))
             first = JC * (jc % 2)
-            per_bank = 4 // n
             for t0 in range(0, 4, per_bank):
                 acc = ps.tile([P, per_bank, JC * n], F32, name=f"y_ps{jc}{t0}", tag="dy", bufs=4)
                 for b in range(2):
@@ -329,10 +327,12 @@ def tile_list_fraud_lowrank_cross_kernel(
                         mm(acc[:, k, :], wn_q[b][0][:, jcols(t0 + k)], wn_q[b][1][:, jcols(t0 + k)], h_q[b][:, cols],
                            h_s[b][:, cols], b == 0 and k == 0, b == 1 and k == per_bank - 1)
                 for k in range(per_bank):
-                    nc.scalar.activation(
-                        out=y_sb[jc // 2][:, t0 + k, first : first + JC * n], in_=acc[:, k, :], func=ACT.Identity,
-                        bias=bn_sb[:, t0 + k : t0 + k + 1],
-                    )
+                    dst = y_sb[jc // 2][:, t0 + k, first : first + JC * n]
+                    bias = bn_sb[:, t0 + k : t0 + k + 1]
+                    if jc == 3 and t0 > 0:
+                        nc.vector.tensor_scalar(out=dst, in0=acc[:, k, :], scalar1=bias, scalar2=None, op0=ALU.add)
+                    else:
+                        nc.scalar.activation(out=dst, in_=acc[:, k, :], func=ACT.Identity, bias=bias)
             nc.sync.dma_start(out=out_rows[:, :, cols], in_=y_sb[jc // 2][:, :, first : first + JC * n])
 
         def round_y(jc, n):
@@ -347,12 +347,12 @@ def tile_list_fraud_lowrank_cross_kernel(
             first = 4 * JC * (jc % 2)
             quantize(y_q[:, cols], y_s[:, cols], y_bf[jc // 2][:, first : first + 4 * JC * n])
 
-        project(0, 2)
+        project(0, 2, 2)
         quantize_h(1, 2, 1)
-        project(2, 1)
+        project(2, 1, 4)
         add_skip(1, 3, prod[1][:, :, jcols(3)])
         quantize_h(1, 3, 1)
-        project(3, 1)
+        project(3, 1, 2)
         round_y(0, 2)
         quantize_y(0, 2)
         nc.sync.dma_start(out=out_words[:, jcols(0, 256)], in_=y_q[:, jcols(0, 256)].bitcast(I32))

import math
from contextlib import ExitStack

import concourse.mybir as mybir
from concourse.masks import make_identity

K, R, H, N, T, S = 1024, 512, 1024, 512, 2048, 512
FLOPS = 2 * S * (K * R + R * H + 2 * K * H + H * N)

F32 = mybir.dt.float32
BF16 = mybir.dt.bfloat16
I32 = mybir.dt.int32
U32 = mybir.dt.uint32
U16 = mybir.dt.uint16
U8 = mybir.dt.uint8
FP8X4 = mybir.dt.float8_e4m3fn_x4
FP4X4 = mybir.dt.float4_e2m1fn_x4
ACT = mybir.ActivationFunctionType
ALU = mybir.AluOpType

P = 128
KP = 512
JC = 128
WU1, WS1, WN = "s", "v", ("s", "s")
BYTES_OF = {F32: 4, I32: 4, U32: 4, BF16: 2, U8: 1}


def tile_list_fraud_lowrank_cross_kernel(
    tc, tab_words, tab_scales, offs, wd, wu, bu, wv_words, wv_scales, ws_words, ws_scales, wn, bn, out_0, out_1, out_2
):
    nc = tc.nc
    with ExitStack() as ctx:
        held = ctx.enter_context(tc.tile_pool(name="held", bufs=1))
        sb = ctx.enter_context(tc.tile_pool(name="sb", bufs=1))
        ps = ctx.enter_context(tc.psum_pool(name="ps", bufs=1))

        place = {"end": 0}

        def tile(shape, dtype, name, over=None, at=0):
            if over is None:
                place[name] = place["end"]
                place["end"] = place[name] + 64 * math.ceil(math.prod(shape[1:]) * BYTES_OF[dtype] / 64)
            else:
                place[name] = place[over] + at
            return sb.tile(shape, dtype, name=name, align_bytes=64, offset=place[name])

        def copy(eng, out, in_):
            if eng == "v":
                nc.vector.tensor_copy(out=out, in_=in_)
            elif eng == "s":
                nc.scalar.copy(out=out, in_=in_)
            else:
                nc.gpsimd.tensor_scalar(out=out, in0=in_, scalar1=1.0, scalar2=0.0, op0=ALU.mult, op1=ALU.add)

        def move(eng, out, in_):
            if eng == "v":
                nc.vector.tensor_copy(out=out.bitcast(I32), in_=in_.bitcast(I32))
            else:
                nc.scalar.copy(out=out.bitcast(U32), in_=in_.bitcast(U32))

        def quantize(codes, scales, in_):
            nc.vector.quantize_mx(out=codes.bitcast(FP8X4), scales=scales, in_=in_)

        offsets = held.tile([P, S // 16], U16, name="offsets")
        nc.sync.dma_start(offsets[:], offs)

        tab_sc = tile([P, 2 * T], U8, "tab_sc")
        w_sc_raw = tile([P, 2 * H], U8, "w_sc_raw")
        w_sc = tile([P, 2 * H], U8, "w_sc")
        nc.vector.memset(tab_sc[:].bitcast(I32), 0)
        nc.vector.memset(w_sc_raw[:].bitcast(I32), 0)

        def load_scales(queue, dst, row0, src):
            for r in range(4):
                queue.dma_start(
                    out=dst[row0 + r : P : 32, :].bitcast(I32).rearrange("q (a n) -> q a n", a=2),
                    in_=src.bitcast(I32).rearrange("a (q r) n -> r q a n", r=4)[r],
                )

        tab_sc_raw = tile([P, 2 * T], U8, "tab_sc_raw")
        load_scales(nc.sync, tab_sc_raw, 0, tab_scales)
        wd_raw = [tile([P, 4, R], F32, f"wd_raw{a}") for a in range(2)]
        for a in range(2):
            nc.sync.dma_start(out=wd_raw[a][:], in_=wd[KP * a : KP * (a + 1), :].rearrange("(p j) c -> p j c", j=4))
        tab_w = [tile([P, T], U32, f"tab_w{a}") for a in range(2)]
        for a in range(2):
            nc.sync.dma_start(out=tab_w[a][:].bitcast(I32), in_=tab_words[a].rearrange("p n t -> p (n t)").bitcast(I32))

        bu_rows = tile([P, 2 * P], F32, "bu_rows")
        nc.gpsimd.memset(bu_rows[:], 0.0)
        nc.scalar.dma_start(
            out=bu_rows[0:4, :].rearrange("t (g i) -> t g i", i=8), in_=bu.rearrange("(g t i) -> t g i", t=4, i=8)
        )
        ident = tile([P, P], F32, "ident")
        make_identity(nc, ident[:])
        load_scales(nc.gpsimd, w_sc_raw, 0, wv_scales)
        load_scales(nc.gpsimd, w_sc_raw, 4, ws_scales)
        bn_sb = tile([P, 4], F32, "bn_sb")
        nc.gpsimd.dma_start(out=bn_sb[:], in_=bn.rearrange("(p t) -> p t", t=4))

        wu_raw0 = [tile([P, 4, KP // 2], F32, f"wu_raw0{half}") for half in range(2)]
        wu_raw1 = tile([P, 4, KP], F32, "wu_raw1")
        wu_rows = wu.rearrange("(p j) c -> p j c", j=4)
        wv_raw = [tile([P, 2, KP // 2], U32, f"wv_raw{b}") for b in range(2)]
        ws_raw = [tile([P, 2, KP], U32, f"ws_raw{b}") for b in range(2)]
        for b in range(2):
            nc.sync.dma_start(
                out=wv_raw[b][:].bitcast(I32),
                in_=wv_words[:, :, 2 * KP * b : 2 * KP * (b + 1)].bitcast(I32).rearrange("a p n -> p a n"),
            )
            if b == 0:
                for half in range(2):
                    nc.sync.dma_start(out=wu_raw0[half][:], in_=wu_rows[:, :, 256 * half : 256 * (half + 1)])
            else:
                nc.sync.dma_start(out=wu_raw1[:], in_=wu_rows[:, :, KP:])
            nc.sync.dma_start(
                out=ws_raw[b][:].bitcast(I32),
                in_=ws_words[:, :, KP * b : KP * (b + 1), :].rearrange("a p n t -> p a (n t)").bitcast(I32),
            )
        wn_raw = [tile([P, 4, N], F32, f"wn_raw{b}") for b in range(2)]
        for b in range(2):
            rows = wn[KP * b : KP * (b + 1), :].rearrange("(g t i) n -> t g i n", t=4, i=8)
            for t in range(4):
                nc.sync.dma_start(out=wn_raw[b][:, t, :], in_=rows[t])

        bu_ps = ps.tile([P, 2, P], F32, name="bu_ps", tag="ring", bufs=4)
        for b in range(2):
            nc.tensor.transpose(bu_ps[:, b, :], bu_rows[:, P * b : P * (b + 1)], ident[:])
        bu_sb = tile([P, 2, 4], F32, "bu_sb")
        nc.scalar.activation(out=bu_sb[:], in_=bu_ps[:, :, 0:4], func=ACT.Copy)

        def dealt_weight(engs, raw, name, over=None, at=0):
            grouped = tile([P, 4 * KP], BF16, name + "_bf", over, at)
            dst = grouped[:].rearrange("p (u v m j) -> p u m j v", u=2, v=2, j=4)
            src = raw[:].rearrange("p j (m u v) -> p u m j v", u=2, v=2)
            if len(engs) == 1:
                copy(engs, dst, src)
            else:
                for u in range(2):
                    copy(engs[u], dst[:, u], src[:, u])
            return grouped

        def quantize_whole(grouped, name):
            codes = tile([P, KP], U32, name + "_q")
            scales = tile([P, KP], U8, name + "_s")
            quantize(codes[:], scales[:], grouped[:])
            return codes, scales

        for q in range(4):
            live = slice(32 * q, 32 * q + 4)
            nc.vector.tensor_copy(out=tab_sc[live, :].bitcast(I32), in_=tab_sc_raw[live, :].bitcast(I32))
        g_sc = [tile([P, S], U8, f"g_sc{a}") for a in range(2)]
        for a in range(2):
            nc.vector.tensor_copy(g_sc[a][:], tab_sc[:, T * a : T * (a + 1)].indirect(offsets[:]))
        wd_bf = [dealt_weight("s", wd_raw[0], "wd0"), dealt_weight("sv", wd_raw[1], "wd1")]
        wd_q = [quantize_whole(wd_bf[a], f"wd{a}") for a in range(2)]

        g_w = [tile([P, S], U32, f"g_w{a}") for a in range(2)]
        for a in range(2):
            for half in range(2):
                nc.vector.tensor_copy(
                    g_w[a][:, 256 * half : 256 * (half + 1)],
                    tab_w[a][:].indirect(offsets[:, 16 * half : 16 * (half + 1)]),
                )

        nc.vector.tensor_copy(
            out=w_sc[:].bitcast(I32).rearrange("p (e t g i) -> p e t g i", t=4, g=16, i=2),
            in_=w_sc_raw[:].bitcast(I32).rearrange("p (e g t i) -> p e t g i", t=4, g=16, i=2),
        )

        def mm(out, lhs, lhs_s, rhs, rhs_s, start, stop, lhs_dt=FP8X4):
            nc.tensor.matmul_mx(
                out=out, lhsT=lhs.bitcast(lhs_dt), lhsT_scale=lhs_s, rhs=rhs.bitcast(FP8X4), rhs_scale=rhs_s,
                start=start, stop=stop,
            )

        def jcols(jc, width=JC):
            return slice(width * jc, width * (jc + 1))

        d_ps = [ps.tile([P, 4, JC], F32, name=f"d_ps{jc}", tag="dy", bufs=4) for jc in range(4)]
        for a in range(2):
            for jc in range(4):
                for t in range(4):
                    mm(d_ps[jc][:, t, :], wd_q[a][0][:, jcols(t)], wd_q[a][1][:, jcols(t)],
                       g_w[a][:, jcols(jc)], g_sc[a][:, jcols(jc)], a == 0 and t == 0, a == 1 and t == 3)
        d_bf = [tile([P, 8 * JC], BF16, f"d_bf{half}") for half in range(2)]
        for jc in range(4):
            nc.scalar.activation(
                out=d_bf[jc // 2][:, jcols(jc % 2, 4 * JC)].rearrange("p (j t) -> p j t", t=4), in_=d_ps[jc][:].rearrange("p t j -> p j t"),
                func=ACT.Relu,
            )
        d_q = tile([P, S], U32, "d_q")
        d_s = tile([P, S], U8, "d_s")

        def quantize_d(half):
            quantize(d_q[:, jcols(half, 256)], d_s[:, jcols(half, 256)], d_bf[half][:])

        wu_q = [tile([P, KP], U32, f"wu_q{b}") for b in range(2)]
        wu_s = [tile([P, KP], U8, f"wu_s{b}") for b in range(2)]
        val = [[tile([P, S], F32, f"val{b}{t}") for t in range(4)] for b in range(2)]
        wu_bf = [
            [tile([P, 2 * KP], BF16, f"wu_bf0{u}", "tab_w1", 2048 * u) for u in range(2)],
            [tile([P, 2 * KP], BF16, f"wu_bf1{u}", f"val0{u + 1}") for u in range(2)],
        ]

        def cast_wu(eng, b, t):
            copy(
                eng,
                wu_bf[b][t // 2][:, jcols(t % 2, KP)].rearrange("p (g u v j) -> p g u j v", u=4, v=2, j=4),
                wu_raw1[:].rearrange("p j (g t i) -> p t g j i", t=4, i=8)[:, t].rearrange("p g j (u v) -> p g u j v", v=2),
            )

        def cast_wu0(half, u):
            nc.vector.tensor_copy(
                out=wu_bf[0][u][:].rearrange("p (v h g i j) -> p h v g i j", v=2, h=2, i=8, j=4)[:, half],
                in_=wu_raw0[half][:].rearrange("p j (g u v i) -> p u v g i j", u=2, v=2, i=8)[:, u],
            )

        def quantize_wu(b, u):
            quantize(wu_q[b][:, jcols(u, 256)], wu_s[b][:, jcols(u, 256)], wu_bf[b][u][:])

        wv_p = [tile([P, 4 * KP], U8, "wv_p0", "tab_w1", 4096), tile([P, 4 * KP], U8, "wv_p1", "val00")]
        ws_p = [tile([P, 2 * KP], U32, f"ws_p{b}", "d_bf0") for b in range(2)]

        def deal_wv(eng, b):
            move(eng, wv_p[b][:].bitcast(U32).rearrange("p (a t g i) -> p a t g i", a=2, t=4, i=4),
                 wv_raw[b][:].rearrange("p a (g t i) -> p a t g i", t=4, i=4))

        def deal_ws(eng, b):
            move(eng, ws_p[b][:].rearrange("p (a t g i) -> p a t g i", a=2, t=4, i=8),
                 ws_raw[b][:].rearrange("p a (g t i) -> p a t g i", t=4, i=8))

        def value(b, t):
            acc = ps.tile([P, S], F32, name=f"val_ps{b}{t}", tag="dy", bufs=4)
            for a in range(2):
                c0 = KP * a + JC * t
                s0 = H * a + KP * b + JC * t
                mm(acc[:], wv_p[b][:, 2 * c0 : 2 * (c0 + JC)], w_sc[:, s0 : s0 + JC], g_w[a][:], g_sc[a][:],
                   a == 0, a == 1, lhs_dt=FP4X4)
            nc.scalar.copy(out=val[b][t][:], in_=acc[:])

        def cross(b, t, j0, width, dst):
            cols = slice(j0, j0 + width)
            acc = ps.tile([P, width], F32, name=f"up_ps{b}{t}{j0}", tag="ring", bufs=4)
            mm(acc[:], wu_q[b][:, jcols(t)], wu_s[b][:, jcols(t)], d_q[:, cols], d_s[:, cols], True, True)
            nc.vector.scalar_tensor_tensor(
                out=dst[:, t, :], in0=acc[:], scalar=bu_sb[:, b, t : t + 1], in1=val[b][t][:, cols],
                op0=ALU.add, op1=ALU.mult,
            )

        h_bf = [[tile([P, 8 * JC], BF16, f"h_bf{b}{half}") for half in range(2)] for b in range(2)]
        h_q = [tile([P, S], U32, f"h_q{b}") for b in range(2)]
        h_s = [tile([P, S], U8, f"h_s{b}") for b in range(2)]

        def add_skip(b, jc, src):
            acc = ps.tile([P, 4, JC], F32, name=f"skip_ps{b}{jc}", tag="ring", bufs=4)
            for t in range(4):
                for a in range(2):
                    c0 = KP * a + JC * t
                    s0 = H * a + KP * b + JC * t
                    mm(acc[:, t, :], ws_p[b][:, c0 : c0 + JC], w_sc[4:P, s0 : s0 + JC], g_w[a][:, jcols(jc)],
                       g_sc[a][:, jcols(jc)], a == 0, a == 1)
            nc.vector.tensor_tensor(
                out=h_bf[b][jc // 2][:, jcols(jc % 2, 4 * JC)].rearrange("p (c i t) -> p c t i", i=2, t=4),
                in0=acc[:].rearrange("p t (c i) -> p c t i", i=2),
                in1=src.rearrange("p t (c i) -> p c t i", i=2),
                op=ALU.add,
            )

        def quantize_h(b, jc, n):
            cols = slice(JC * jc, JC * (jc + n))
            first = 4 * JC * (jc % 2)
            quantize(h_q[b][:, cols], h_s[b][:, cols], h_bf[b][jc // 2][:, first : first + 4 * JC * n])

        deal_wv("v", 0)
        cast_wu0(0, 0)
        cast_wu0(0, 1)
        quantize_d(0)
        cast_wu0(1, 0)
        cast_wu0(1, 1)
        quantize_wu(0, 0)
        quantize_d(1)
        quantize_wu(0, 1)
        deal_ws("v", 0)

        prod = [tile([P, 4, S], F32, f"prod{b}") for b in range(2)]
        for t in range(4):
            value(0, t)
            cross(0, t, 0, S, prod[0])
        deal_wv("s", 1)
        for t in range(4):
            cast_wu(WU1, 1, t)
        for jc in range(4):
            add_skip(0, jc, prod[0][:, :, jcols(jc)])
            if jc == 2:
                quantize_h(0, 0, 2)
            if jc % 2 == 1:
                quantize_wu(1, jc // 2)
            value(1, jc)
        deal_ws(WS1, 1)
        quantize_h(0, 2, 2)

        wn_bf = [dealt_weight(WN[b], wn_raw[b], f"wn{b}", "prod0", 4096 * b) for b in range(2)]
        for t in range(4):
            cross(1, t, 0, S, prod[1])
        wn_q = [quantize_whole(wn_bf[0], "wn0")]
        add_skip(1, 0, prod[1][:, :, jcols(0)])
        add_skip(1, 1, prod[1][:, :, jcols(1)])
        wn_q.append(quantize_whole(wn_bf[1], "wn1"))
        quantize_h(1, 0, 2)
        add_skip(1, 2, prod[1][:, :, jcols(2)])

        y_sb = [tile([P, 4, S // 2], F32, f"y_sb{half}") for half in range(2)]
        y_bf = [tile([P, 8 * JC], BF16, f"y_bf{half}") for half in range(2)]
        y_q = tile([P, S], U32, "y_q")
        y_s = tile([P, S], U8, "y_s")
        out_rows = out_0.rearrange("(p t) j -> p t j", t=4)
        out_words = out_1[0].rearrange("p m t -> p (m t)").bitcast(I32)

        def project(jc, n, per_bank):
            cols = slice(JC * jc, JC * (jc + n))
            first = JC * (jc % 2)
            for t0 in range(0, 4, per_bank):
                acc = ps.tile([P, per_bank, JC * n], F32, name=f"y_ps{jc}{t0}", tag="dy", bufs=4)
                for b in range(2):
                    for k in range(per_bank):
                        mm(acc[:, k, :], wn_q[b][0][:, jcols(t0 + k)], wn_q[b][1][:, jcols(t0 + k)], h_q[b][:, cols],
                           h_s[b][:, cols], b == 0 and k == 0, b == 1 and k == per_bank - 1)
                for k in range(per_bank):
                    dst = y_sb[jc // 2][:, t0 + k, first : first + JC * n]
                    bias = bn_sb[:, t0 + k : t0 + k + 1]
                    if jc == 3 and t0 > 0:
                        nc.vector.tensor_scalar(out=dst, in0=acc[:, k, :], scalar1=bias, scalar2=None, op0=ALU.add)
                    else:
                        nc.scalar.activation(out=dst, in_=acc[:, k, :], func=ACT.Identity, bias=bias)
            nc.sync.dma_start(out=out_rows[:, :, cols], in_=y_sb[jc // 2][:, :, first : first + JC * n])

        def round_y(jc, n):
            first = JC * (jc % 2)
            nc.vector.tensor_copy(
                out=y_bf[jc // 2][:, 4 * first : 4 * (first + JC * n)].rearrange("p (c i t) -> p c t i", i=2, t=4),
                in_=y_sb[jc // 2][:, :, first : first + JC * n].rearrange("p t (c i) -> p c t i", i=2),
            )

        def quantize_y(jc, n):
            cols = slice(JC * jc, JC * (jc + n))
            first = 4 * JC * (jc % 2)
            quantize(y_q[:, cols], y_s[:, cols], y_bf[jc // 2][:, first : first + 4 * JC * n])

        project(0, 2, 2)
        quantize_h(1, 2, 1)
        project(2, 1, 4)
        add_skip(1, 3, prod[1][:, :, jcols(3)])
        quantize_h(1, 3, 1)
        project(3, 1, 2)
        round_y(0, 2)
        quantize_y(0, 2)
        nc.sync.dma_start(out=out_words[:, jcols(0, 256)], in_=y_q[:, jcols(0, 256)].bitcast(I32))
        round_y(2, 1)
        quantize_y(2, 1)
        round_y(3, 1)
        quantize_y(3, 1)
        nc.scalar.dma_start(out=out_words[:, jcols(1, 256)], in_=y_q[:, jcols(1, 256)].bitcast(I32))
        for q in range(4):
            queue = nc.scalar if q % 2 == 0 else nc.sync
            queue.dma_start(
                out=out_2[0].bitcast(I32).rearrange("(q r) n -> r q n", r=4)[q], in_=y_s[q:P:32, :].bitcast(I32)
            )
